import numpy as np, ml_dtypes
CORES = [24,25,26,27,28,29,30,31]
N = 8
import mx_ref
BF = ml_dtypes.bfloat16
def entries(a):
    return np.ascontiguousarray(a.T).reshape(-1)
def table(e):
    return np.ascontiguousarray(np.reshape(e, (-1, 16)).T).astype(np.int32)
def gentries(a):
    return np.ascontiguousarray(a.reshape(8, 16, -1).transpose(0, 2, 1)).reshape(8, -1)
def gtable(e):
    e = np.asarray(e); return np.ascontiguousarray(e.reshape(8, -1, 16).transpose(0, 2, 1)).reshape(128, -1).astype(np.int32)
def gcols(t, e):
    v = np.concatenate([t.reshape(8, 16, -1, 4), np.zeros((8, 16, 1, 4), BF)], axis=2)
    return np.ascontiguousarray(np.stack([v[g][:, e[g]] for g in range(8)])).reshape(128, -1)
def tile(rs):
    return np.stack(rs, axis=2).reshape(128, -1).astype(BF)
def pick(q, e):
    c = np.concatenate([q[0].reshape(128, -1, 4), np.zeros((128, 1, 4), np.uint8)], axis=1); s = np.concatenate([q[1], np.ones((16, 1), np.uint8)], axis=1)
    return (np.ascontiguousarray(c[:, e].reshape(128, -1)), np.ascontiguousarray(s[:, e]))
def join(*qs):
    return (np.concatenate([q[0] for q in qs], axis=1), np.concatenate([q[1] for q in qs], axis=1))
def put(q, e, v):
    c, s = q[0].reshape(128, -1, 4).copy(), q[1].copy(); c[:, e] = v[0].reshape(128, -1, 4); s[:, e] = v[1]
    return (c.reshape(128, -1), s)
def pk(c, s):
    return (np.ascontiguousarray(c), mx_ref.live(s))
def emit(q):
    return q[0], q[1]
def packed(v, rng):
    q = [mx_ref.quantize(np.ascontiguousarray(v[r])) for r in range(N)]
    return np.stack([a for a, b in q]), np.stack([mx_ref.plane(b, rng) for a, b in q])
def values_of_codes():
    e, c = np.zeros((128, 128, 4), np.float32), np.zeros((128, 2, 4), np.uint8)
    e[np.arange(128), np.arange(128), 0] = 1
    c[:127, :, 0] = np.arange(256).reshape(2, 128).T[:127]
    return mx_ref.matmul(mx_ref.quantize(e.reshape(128, 512).astype(BF)), (c.reshape(128, 8), np.full((16, 2), 127, np.uint8))).T.reshape(-1).astype(np.float64)
CODE_VALUE, SCALE_VALUE = values_of_codes(), 2.0 ** (np.arange(256) - 127.0)
def decode(q):
    return (CODE_VALUE[q[0]].reshape(16, 8, -1, 4) * SCALE_VALUE[q[1]][:, None, :, None] + 0.0).reshape(128, -1).astype(np.float32)
def f(rng, *shape):
    return mx_ref.flush((rng.standard_normal(shape, dtype=np.float32) * np.exp2(rng.integers(-2, 3, shape[:-1] + (1,)))).astype(BF))
def wide(rng, *shape, cols=0):
    v = rng.standard_normal(shape, dtype=np.float32) * np.exp2(rng.integers(-12, 13, shape)).astype(np.float32)
    if cols: v *= np.repeat(np.exp2(rng.integers(-cols, cols + 1, shape[:-2] + (1, shape[-1] // 4))) * (rng.random(shape[:-2] + (1, shape[-1] // 4)) > 0.0625), 4, axis=-1).astype(np.float32)
    return mx_ref.flush(v.astype(BF))
C = 384
STEP = [1, 2, 4]
def numbers_of(rng):
    return {"x": np.array(f(rng, N, 128, 4 * C)), "u": np.array(f(rng, N, 128, 512)), "v": np.array(f(rng, N, 128, 512))}
def orders(rng):
    return rng.permuted(np.tile(np.arange(C), (N, 1)), axis=1)
def pairing(rng):
    p = rng.permuted(np.tile(np.arange(C), (N, 8, 1)), axis=2)
    m = np.zeros((N, 8, C), np.int64)
    np.put_along_axis(m, p[:, :, ::2], p[:, :, 1::2], axis=2)
    np.put_along_axis(m, p[:, :, 1::2], p[:, :, ::2], axis=2)
    return m
def stored(a, t, m):
    return {"la": np.stack([table(a[r]) for r in range(N)]), "lb": np.stack([table(t[r]) for r in range(N)]), "mt": np.stack([gtable(m[r]) for r in range(N)])}
def lists(rng):
    return stored(orders(rng), orders(rng), pairing(rng))
def layers(rng, still=[]):
    w = np.array(f(rng, N, 128, 2048)).reshape(N, 8, 16, 4, 8, 16, 4)
    for i in still:
        w[:, :, i] = 0
        w[:, :, :, :, :, i] = 0
    return w
def weights(rng, w):
    c, p = packed(np.ascontiguousarray(w).reshape(N, 128, 2048), rng)
    return {"wc": c, "ws": p}
def setup_inputs(rng):
    return {**numbers_of(rng), **lists(rng), **weights(rng, layers(rng))}
def setup_inputs_ties(rng):
    d = numbers_of(rng)
    m = pairing(rng)
    o = rng.permutation(N)
    k = rng.integers(0, 4, (N, 8, C))
    k[o[1]] += 1
    k[o[2]] = (np.arange(C) > m[o[2]]) == (rng.permutation(8) < 4)[:, None]
    k[o[3]] = 1
    h = rng.permutation(8)
    k[o[3], h[:4], C - 1] = 2
    k[o[3], h[4:], 0] = 0
    x = d["x"].reshape(N, 8, 16, C, 4)
    x[:, :, 0] = 0
    x[:, :, 0, :, 0] = k.astype(np.float32).astype(BF)
    a = np.tile(np.exp2(rng.integers(-3, 4, (1, 8, 1)).astype(np.float32)), (N, 1, C))
    x[:, :, 8:] = 0
    x[:, :, 8, :, 0] = (-1.125 * a).astype(BF)
    x[:, :, 10, :, 0] = (-0.0703125 * a).astype(BF)
    u = d["u"].reshape(N, 128, 128, 4)
    u[:, :, ::16] = 0
    for r in range(N):
        for i in range(0, 128, 16): u[r, i, i, 0] = 0.0 if r == o[0] else -1.0 if r == o[1] else 1.0
    w = layers(rng, [0])
    w[:, :, :, :, :, 8:] = 0
    for g in range(8):
        w[:, g, 8, 0, g, 8, 0] = -28.0
        for b in range(4): w[:, g, 10, b, g, 9, 0] = -2.0 ** (b - 5)
    return {"x": x.reshape(N, 128, 4 * C), "u": u.reshape(N, 128, 512), "v": d["v"], **stored(orders(rng), orders(rng), m), **weights(rng, w)}
def setup_inputs_near(rng):
    d = numbers_of(rng)
    o = np.zeros(N, np.int64)
    for n, r in enumerate(rng.permutation([r for r in range(N) if r < r ^ STEP[0]])):
        e = rng.integers(2)
        o[r], o[r ^ STEP[0]] = n % 2 * 2 + e, n % 2 * 2 + 1 - e
    x = d["x"].astype(np.float32).reshape(N, 8, 16, C, 4)
    x[:, :, 0] = 0
    x[:, :, 8:] = 0
    u = d["u"].reshape(N, 128, 128, 4)
    u[:, :, ::16] = 0
    w = layers(rng, [0, 1, 8, 9, 10, 11, 12, 13, 14, 15])
    for r in range(N):
        c = rng.choice([-1.0, 1.0], (8, 1))
        s = rng.integers(0, 16, (8, C))
        digits = ((s[:, :, None] >> np.arange(4)) & 1) * np.exp2(np.arange(4) - 23.0)
        if o[r] < 2:
            x[r, :, 0, :, 0] = c
            x[r, :, 8] = digits
            x[r, :, 11, :, 0] = 2.0 ** -10
        elif o[r] == 2:
            x[r, :, 8] = digits * rng.choice([-1.0, 1.0], (8, C, 1))
            x[r, :, 1:8] = 0
            x[r, :, 1, :, 0] = rng.choice([-1.0, 1.0], (8, C)) * 2.0 ** -30
            for g in range(8):
                w[r, g, 1, 0, g, 12, 0] = 2.0 ** -8
                w[r, g, 1, 0, g, 13, 0] = 64.0
        else:
            x[r, :, 8, :, 0] = np.where(s < 8, 1.25, 0.0) * 2.0 ** -30 * c
            x[r, :, 9, :, 0] = np.where(s < 8, 0.0, 1.125) * 2.0 ** -30 * c
            for g in rng.permutation(8)[:4]:
                e = rng.choice([-1.0, 1.0], C) * 2.0 ** -30
                x[r, g, 8, :, 0] = 1.25 * e
                x[r, g, 9, :, 0] = -1.125 * e
        at = [0, C - 1, int(rng.integers(C)), int(rng.integers(C))]
        for g, j in zip(rng.permutation(8)[:4], at): x[r, g, 0, j, 0] = 2.0 ** 29 * rng.choice([-1.0, 1.0])
        k = 1.0 if o[r] == 0 else 2.0 ** -30
        for h in range(0, 128, 16):
            u[r, h, h, 0] = k
            if o[r] < 2: u[r, h + 11, h, 0] = k
            if o[r] < 3: u[r, h + 8, h] = k
            else:
                u[r, h + 8, h, 0] = k
                u[r, h + 9, h, 0] = 1.125 * k
                u[r, h + 12, h, 0] = k
    return {"x": x.reshape(N, 128, 4 * C).astype(BF), "u": u.reshape(N, 128, 512), "v": d["v"], **lists(rng), **weights(rng, w)}
def setup_inputs_odd(rng):
    d = numbers_of(rng)
    x = (1.0 + (2 * rng.integers(0, 64, (N, 16, 8, C, 4)) + 1) * 2.0 ** -7) * np.exp2(-rng.integers(0, 7, (N, 16, 8, C, 4)).astype(np.float64)) * rng.choice([-1.0, 1.0], (N, 16, 8, C, 4))
    x[:, :, 0, :, 0] = 1.96875 * 2.0 ** 8 * rng.choice([-1.0, 1.0], (N, 16, C))
    u = d["u"].reshape(N, 16, 8, 128, 4)
    u[:, :, 0, ::16] = 0
    for r in range(N):
        for n, g in enumerate(rng.permutation(8)[:4]):
            x[r, 2 * g, 1, :, 0] = (8 + rng.integers(0, 2, C)) * 2.0 ** (n % 2 - 8)
            u[r, :, :, 16 * g] = 0
            u[r, 2 * g, 1, 16 * g, 0] = 1.0
    return {"x": x.astype(np.float32).reshape(N, 128, 4 * C).astype(BF), "u": u.reshape(N, 128, 512), "v": d["v"], **lists(rng), **weights(rng, layers(rng, [0, 8]))}
def setup_inputs_ends(rng):
    d = numbers_of(rng)
    o, e = rng.permutation(N) % 4, rng.permutation(N) % 4
    x = np.zeros((N, 8, 16, C, 4))
    u = d["u"].astype(np.float32).reshape(N, 128, 128, 4)
    v = np.zeros((N, 128, 512))
    w = np.zeros((N, 128, 4, 128, 4), np.float32)
    still = int(rng.integers(8))
    i = np.arange(128)
    for r in range(N):
        h = rng.permutation(8)
        c = np.where(h < 2, 0.0, h % 2 * 2.0 - 1.0)[None, :, None]
        large = (0.88 + 0.04 * rng.random((8, 16, C, 4))) * 2.0 ** 30
        if o[r] == 0: x[r] = -large
        if o[r] == 1: x[r] = large * rng.choice([-1.0, 1.0], (C, 1))
        if o[r] == 2: x[r] = -(1.0 + 0.125 * rng.integers(0, 8, (8, 16, C, 4))) * 2.0 ** -30
        if o[r] == 3: x[r] = d["x"][r].astype(np.float32).reshape(8, 16, C, 4)[:, :, :1]
        if o[r] < 2: u[r, :, ::16] = c * (0.9 + 0.1 * rng.random((128, 8, 4))) * 2.0 ** 30
        if o[r] == 2: u[r, :, ::16] = c * (1.0 + 0.125 * rng.integers(0, 8, (128, 8, 4))) * 2.0 ** -30
        if o[r] == 3: u[r, :, ::16] *= np.abs(c).astype(np.float32)
        v[r] = rng.choice([-1.0, 1.0], (128, 512)) * (2.0 ** 30 if o[r] < 2 else 2.0 ** -30)
        k = np.array([0.125, 0.25, 0.5])[rng.permutation(8) % 3]
        if o[r] == 2: k[:] = 32.0
        if o[r] == 3: k[k == 0.125] = 2.0 ** -8
        k[still] = 256.0 if o[r] == 2 else 0.0
        for b in range(4): w[r, i, b, i, b] = k[i // 16]
    a, t, m = orders(rng), orders(rng), pairing(rng)
    j = np.arange(C)
    a[e == 0] = j
    t[e == 0] = j
    m[e == 0] = j ^ 1
    a[e == 1] = C - 1 - j
    t[e == 1] = C - 1 - j
    m[e == 1] = C - 1 - j
    a[e == 2] = (j + 1) % C
    t[e == 2] = (j + C - 1) % C
    m[e == 2] = (j + C // 2) % C
    return {"x": x.astype(np.float32).reshape(N, 128, 4 * C).astype(BF), "u": u.reshape(N, 128, 512).astype(BF), "v": v.astype(np.float32).astype(BF), **stored(a, t, m), **weights(rng, w.astype(BF))}
def setup_inputs_spread(rng):
    d = setup_inputs(rng)
    d["x"] = wide(rng, N, 128, 4 * C, cols=6)
    return d
def check_inputs(d):
    b = []
    for k in ("x", "u", "v"):
        a = np.abs(d[k].astype(np.float32))
        if not (np.isfinite(a).all() and ((a == 0) | (a >= 2.0 ** -30) & (a <= 2.0 ** 30)).all()): b.append("a value of " + k)
    none, least, most = [emit(mx_ref.quantize(np.full((128, 16), k, np.float32).astype(BF)))[1][0, 0] for k in (0.0, 2.0 ** -8, 2.0 ** 8)]
    for r in range(N):
        for k in ("la", "lb"):
            if (np.sort(entries(d[k][r])) != np.arange(C)).any(): b.append(k + ": not every number once")
        m = gentries(d["mt"][r])
        if not ((m >= 0) & (m < C)).all(): b.append("an entry of mt")
        elif (np.take_along_axis(m, m, axis=1) != np.arange(C)).any() or (m == np.arange(C)).any(): b.append("mt: not in pairs")
        if ((d["wc"][r] == 0x7F) | (d["wc"][r] == 0xFF)).any(): b.append("wc: a code that is no number")
        s = mx_ref.live(d["ws"][r])
        if ((s != none) & ((s < least) | (s > most))).any(): b.append("ws: a scale out of range")
        if (((d["wc"][r].reshape(16, 8, 512, 4) & 0x7F) != 0) & (s == none)[:, None, :, None]).any(): b.append("wc: a code other than zero under the scale of zeros")
    return b
def reference(x, u, v, la, lb, mt, wc, ws):
    qu = [mx_ref.quantize(u[r]) for r in range(N)]
    lay = [pk(wc[r], ws[r]) for r in range(N)]
    mate = [gentries(mt[r]) for r in range(N)]
    kept = [[entries(la[r]), entries(lb[r])] for r in range(N)]
    now = [x[r] for r in range(N)]
    here = np.tile(np.arange(C), (8, 1))
    ll = np.zeros((N, 8, C), np.float32)
    for step in STEP:
        went, sent = [], []
        for r in range(N):
            s = mx_ref.matmul(qu[r], mx_ref.quantize(now[r]))[::16] + np.float32(0.0)
            t = np.take_along_axis(s, mate[r], axis=1)
            crossed = np.where(here < mate[r], s < t, t < s)
            e = np.where(crossed, mate[r], here)
            a = [kept[r][0][e[0]], kept[r][1][e[7]]]
            kept[r] = a[:2]
            for g in range(1, 7):
                k = e[g][a[g]]
                a.append(a[g - 1][k[k]])
            went.append(np.stack(a))
            ll[r] = went[r]
            z = mx_ref.quantize(gcols(now[r], went[r]))
            sent.append(mx_ref.quantize(tile([mx_ref.matmul(pick(lay[r], np.arange(128 * b, 128 * b + 128)), z) * np.float32(0.03125) for b in range(4)])))
        made = []
        for r in range(N):
            far = gcols(decode(sent[r ^ step]).astype(BF), went[r][::-1])
            made.append((now[r].astype(np.float32) + far.astype(np.float32)).astype(BF))
        now = made
    y = np.zeros((N, 128, C), np.float32)
    oc, osc = np.zeros((N, 128, 4 * C), np.uint8), np.zeros((N, 16, C), np.uint8)
    for r in range(N):
        q = mx_ref.quantize(now[r])
        y[r] = mx_ref.matmul(mx_ref.quantize(v[r]), q)
        oc[r], osc[r] = emit(q)
    return {"y": y, "ll": ll, "oc": oc, "osc": osc}

@@ -1,0 +1,419 @@
+from concourse.mybir import dt, AluOpType as OP, ActivationFunctionType as AF
+
+C = 384
+HALF = C // 2
+STEP = [1, 2, 4]
+ROW = 416
+NV = 12
+
+SCRATCH = {}
+SEMAPHORES = ["cv", "cs", "ct", "cg"]
+
+
+def _declare():
+    def sb(name, cols, dtype):
+        SCRATCH[name] = ("sbuf", [128, cols], dtype)
+    bf, f32, i32, u16, co, u8 = "bfloat16", "float32", "int32", "uint16", "float8_e4m3fn_x4", "uint8"
+    for n, c in (("xt", 4 * C), ("ut", 512), ("vt", 512), ("zt", 4 * C), ("hg", 4 * C), ("fl", 4 * ROW), ("ones", 512), ("c0", 512),
+                 ("ce", 512), ("cd", 512), ("e0", 512), ("e1", 512), ("e2", 512), ("e3", 512), ("r0", C), ("r0c", C), ("newc", 400), ("idc", C), ("base", 400),
+                 ("new", ROW), ("pa", ROW), ("tr", 8 * ROW), ("lb16", C)):
+        sb(n, c, bf)
+    for b in range(4):
+        sb("xp%d" % b, C, bf)
+        sb("hp%d" % b, C, bf)
+    for k in range(8):
+        sb("f%d" % k, ROW, bf)
+    for n, c in (("idf", 400), ("wsg", C), ("wf", C), ("dl8", C), ("delta", 400), ("tm", 400), ("dab", 400), ("sw", C), ("ns", C), ("ysb", C), ("l32", C),
+                 ("cb", 1), ("cn", 1), ("cm", 1), ("p15", 1), ("c32", 1), ("bs1", 1), ("t1", 1), ("t2", 1), ("bs2", 1), ("k2", 2)):
+        sb(n, c, f32)
+    for n, c in (("mti", 24), ("offi", 24), ("ip", 1), ("b16", 1), ("i15", 1), ("ph", 1), ("ik", 24), ("mi", 26)):
+        sb(n, c, i32)
+    for n, c in (("mt16", 24), ("offa", 24), ("sel", 4), ("ml", 26), ("oa", 26), ("ob", 26), ("lf", 64)):
+        sb(n, c, u16)
+    for k in range(1, 7):
+        sb("ok%d" % k, 26, u16)
+    for n, c in (("xq", C), ("uq", 128), ("vq", 128), ("zq", C), ("hq", C), ("fq", ROW), ("wq", 512), ("ceq", 128), ("cdq", 128),
+                 ("e0q", 128), ("e1q", 128), ("e2q", 128), ("e3q", 128)):
+        sb(n, c, co)
+        sb(n + "s", c, u8)
+    for r in range(3):
+        sb("lr%d" % r, 24, u16)
+        sb("hr%d" % r, C, co)
+        sb("hr%ds" % r, C, u8)
+    for k in range(8):
+        SCRATCH["ps%d" % k] = ("psum", [128, 512], f32)
+    for r in range(3):
+        for n in ("l", "c0", "s0", "c1", "s1"):
+            SEMAPHORES.append("ar%d%s" % (r, n))
+            SEMAPHORES.append("lo%d%s" % (r, n))
+    for n in ("x0", "x1", "mt", "u", "v", "la", "wc", "ws", "mi", "bs", "dl", "st", "out"):
+        SEMAPHORES.append("d_" + n)
+    for r in range(2):
+        SEMAPHORES.append("d_nb%d" % r)
+        SEMAPHORES.append("d_nd%d" % r)
+
+
+_declare()
+
+
+def _span(a, b, s):
+    return slice(a, b) if s == 1 else slice(a, b, s)
+
+
+def _meet(a0, a1, s, b0, b1, t):
+    if a0 >= b1 or b0 >= a1:
+        return False
+    return not (s == t and s > 1 and (a0 - b0) % s)
+
+
+def _builder(g, T):
+    eng = {"v": g.vector, "s": g.scalar, "t": g.tensor, "g": g, "y": g.sync}
+    known = {q: {} for q in eng}
+    hist, cnt, closed = {}, {}, set()
+    serial = [0]
+
+    def ap(r):
+        name, c, p, bits = r
+        p = slice(None) if p == (0, 128, 1) else _span(*p)
+        a = T[name][p, _span(*c)]
+        return a.bitcast(dt.uint8) if bits else a
+
+    def deps(q, reads, writes, matmul=False):
+        found = {}
+        for refs, w in ((reads, False), (writes, True)):
+            for name, c, p, bits in refs:
+                psum = name[:2] == "ps"
+                for (c2, p2, w2, tok, clk, q2, n) in hist.get(name, ()):
+                    if psum:
+                        if q2 == q and (q == "t" or not (w or w2)):
+                            continue
+                    else:
+                        if not (w or w2):
+                            continue
+                        if not (_meet(*c, *c2) and _meet(*p, *p2)):
+                            continue
+                    found[n] = (tok, clk)
+        return [found[n] for n in sorted(found, reverse=True)]
+
+    def wait(q, toks):
+        k = known[q]
+        for (sem, val), clk in toks:
+            if sem in closed or sem[:2] == "d_":
+                val = cnt[sem]
+                closed.add(sem)
+            if k.get(sem, 0) >= val:
+                continue
+            eng[q].wait_ge(T.sem[sem], val)
+            k[sem] = val
+            for s2, v2 in clk.items():
+                if k.get(s2, 0) < v2:
+                    k[s2] = v2
+
+    def note(q, reads, writes, tok):
+        serial[0] += 1
+        clk = dict(known[q])
+        for refs, w in ((reads, False), (writes, True)):
+            for name, c, p, bits in refs:
+                h = hist.setdefault(name, [])
+                if w and name[:2] != "ps":
+                    h[:] = [e for e in h if not (c[0] <= e[0][0] and e[0][1] <= c[1] and c[2] == 1 and p == (0, 128, 1))]
+                h.append((c, p, w, tok, clk, q, serial[0]))
+
+    def issue(q, fn, reads, writes, sem=None, inc=1):
+        wait(q, deps(q, reads, writes))
+        sem = sem or "c" + q
+        assert sem not in closed, sem
+        cnt[sem] = cnt.get(sem, 0) + inc
+        fn(eng[q]).then_inc(T.sem[sem], inc)
+        note(q, reads, writes, (sem, cnt[sem]))
+
+    def remote(out, src, dst, ars, los, topo, core):
+        wait("g", deps("g", [src], []))
+        rid, pid, _ = topo.addr(dst)
+        n = len(topo.engines(core, dst))
+        g.remote_dma(ap(out), ap(src), T.sem[ars], T.sem[los], pid, rid, topo.mask(core, dst))
+        cnt[los] = n
+        note("g", [src], [], (los, n))
+
+    def arrives(out, sem, n):
+        serial[0] += 1
+        cnt[sem] = n
+        hist.setdefault(out[0], []).append((out[1], out[2], True, (sem, n), {}, "remote", serial[0]))
+
+    def finish():
+        for sem in sorted(cnt):
+            if known["g"].get(sem, 0) < cnt[sem]:
+                g.wait_ge(T.sem[sem], cnt[sem])
+                known["g"][sem] = cnt[sem]
+
+    return ap, issue, remote, arrives, finish
+
+
+def rank_program(g, core, T, topo):
+    rank = T.rank_of(core)
+    if rank is None:
+        return
+    ap, issue, remote, arrives, finish = _builder(g, T)
+
+    def R(name, c0, c1, cs=1, p0=0, p1=128, ps=1):
+        return (name, (c0, c1, cs), (p0, p1, ps), False)
+
+    def B(name, c0, c1):
+        return (name, (c0, c1, 1), (0, 128, 1), True)
+
+    def P(name, p0=0, p1=128):
+        return R(name, 0, 1, 1, p0, p1)
+
+    def dma(q, sem, out, in_, ext_in=None, ext_out=None):
+        issue(q, lambda e: e.dma_start(ext_out if ext_out is not None else ap(out), ext_in if ext_in is not None else ap(in_)),
+              [in_] if in_ else [], [out] if out else [], "d_" + sem, 16)
+
+    def val(s):
+        return ap(s) if isinstance(s, tuple) else s
+
+    def memset(r, c):
+        issue("v", lambda e: e.memset(ap(r), c), [], [r])
+
+    def tt(out, a, b, op, off=None):
+        def fn(e):
+            x = ap(a)
+            return e.tensor_tensor(ap(out), x.indirect(ap(off)) if off else x, ap(b), op)
+        issue("v", fn, [a, b] + ([off] if off else []), [out])
+
+    def ts(out, a, s1, s2, op0, op1=None, off=None):
+        def fn(e):
+            x = ap(a)
+            x = x.indirect(ap(off)) if off else x
+            if op1 is None:
+                return e.tensor_scalar(ap(out), x, val(s1), None, op0)
+            return e.tensor_scalar(ap(out), x, val(s1), val(s2), op0, op1)
+        issue("v", fn, [a] + [s for s in (s1, s2, off) if isinstance(s, tuple)], [out])
+
+    def copy(q, out, a, off=None, scale=None, bias=None):
+        def fn(e):
+            x = ap(a)
+            x = x.indirect(ap(off)) if off else x
+            if q == "v":
+                return e.tensor_copy(ap(out), x)
+            if bias is not None:
+                return e.activation(ap(out), x, AF.Identity, bias=val(bias), scale=1.0 if scale is None else scale)
+            return e.activation(ap(out), x, AF.Copy) if scale is None else e.activation(ap(out), x, AF.Copy, scale=scale)
+        issue(q, fn, [a] + [r for r in (off, bias) if isinstance(r, tuple)], [out])
+
+    def turn(out, a):
+        issue("v", lambda e: e.transpose(ap(out), ap(a)), [a], [out])
+
+    def quant(name, c0, c1, tile, t0):
+        q, s, t = R(name, c0, c1), R(name + "s", c0, c1), R(tile, t0, t0 + 4 * (c1 - c0))
+        issue("v", lambda e: e.quantize_mx(ap(q), ap(s), ap(t)), [t], [q, s])
+
+    def mm(bank, n, lhs, l0, rhs, c0, start=True, stop=True):
+        out = R("ps%d" % bank, 0, n)
+        a, sa, b, sb = R(lhs, l0, l0 + 128), R(lhs + "s", l0, l0 + 128), R(rhs, c0, c0 + n), R(rhs + "s", c0, c0 + n)
+        issue("t", lambda e: e.matmul_mx(ap(out), ap(a), ap(sa), ap(b), ap(sb), start, stop), [a, sa, b, sb], [out])
+
+    def iota(r, pattern, base, mult, flag=False):
+        if flag:
+            issue("g", lambda e: e.iota(ap(r), pattern, base, mult, allow_small_or_imprecise_dtypes=True), [], [r])
+        else:
+            issue("g", lambda e: e.iota(ap(r), pattern, base, mult), [], [r])
+
+    def select(out, in_, pattern, base, mult):
+        issue("g", lambda e: e.affine_select(ap(out), ap(in_), pattern, OP.is_equal, 0.0, base, mult), [in_], [out])
+
+    full = R("tr", 0, 8 * ROW)
+    chunks = [(0, HALF), (HALF, C)]
+
+    dma("y", "mt", R("mti", 0, 24), None, T.mt[:, :])
+    for k, (a, b) in enumerate(chunks):
+        dma("y", "x%d" % k, R("xt", 4 * a, 4 * b), None, T.x[:, 4 * a:4 * b])
+    dma("s", "u", R("ut", 0, 512), None, T.u[:, :])
+
+    iota(R("ip", 0, 1), [[0, 1]], 0, 1)
+    iota(R("ik", 0, 24), [[16, 24]], 0, 0)
+    iota(R("idf", 0, 400), [[1, 400]], -HALF, 0, True)
+    memset(R("ones", 0, 512), 1.0)
+    ts(P("i15"), P("ip"), 15, None, OP.bitwise_and)
+    ts(P("b16"), P("ip"), 16, None, OP.bitwise_and)
+    ts(P("ph"), P("ip"), 4, None, OP.logical_shift_right)
+    copy("v", P("p15"), P("i15"))
+    ts(R("offi", 0, 24), R("ik", 0, 24), P("p15"), None, OP.add)
+    dma("s", "la", R("offi", 0, 24, 1, 0, 16), None, T.la[:, :])
+    dma("s", "la", R("offi", 0, 24, 1, 112, 128), None, T.lb[:, :])
+    ts(P("cb"), P("b16"), -1.0, 208.0, OP.mult, OP.add)
+    ts(P("cm"), P("b16"), -16.0, None, OP.add)
+    ts(P("cn"), P("b16"), -1.0, 16.0, OP.mult, OP.add)
+    ts(P("c32"), P("b16"), -1.0, 32.0, OP.mult, OP.add)
+    ts(P("bs1"), P("ph"), float(ROW), P("c32"), OP.mult, OP.add)
+    ts(P("bs2"), P("ph"), -float(ROW), P("c32"), OP.mult, OP.add)
+    ts(P("bs2"), P("bs2"), 7.0 * ROW, None, OP.add)
+    ts(P("t1"), P("ph"), 0.0, 8.0, OP.is_gt, OP.mult)
+    ts(P("t2"), P("ph"), 7.0, 8.0, OP.is_lt, OP.mult)
+    tt(P("bs1"), P("bs1"), P("t1"), OP.add)
+    tt(P("bs2"), P("bs2"), P("t2"), OP.add)
+    ts(R("k2", 0, 2), R("ik", 0, 2), P("p15"), 23.0, OP.add, OP.min)
+    ts(R("sel", 0, 2), R("k2", 0, 2), 16.0, P("bs1"), OP.mult, OP.add)
+    ts(R("sel", 2, 4), R("k2", 0, 2), 16.0, P("bs2"), OP.mult, OP.add)
+    copy("s", R("idc", 0, C), R("idf", 0, C))
+    copy("s", R("base", 0, 400), R("idf", 0, 400), bias=P("cm"))
+    memset(R("delta", 0, 400), 0.0)
+    memset(R("mi", 0, 26), 0)
+    memset(R("fl", 0, 4 * ROW), 0.0)
+    memset(R("new", 0, 16), 0.0)
+    for k in range(1, 8):
+        memset(R("f%d" % k, 0, 16), 0.0)
+    dma("y", "wc", ("wq", (0, 512, 1), (0, 128, 1), True), None, T.wc[:, :])
+    dma("y", "ws", R("wqs", 0, 512), None, T.ws[:, :])
+    for h in range(8):
+        o = 1 - h % 2
+        m = 0 if h < 4 else 112
+        dma("y", "mi", R("mi", o, o + 24, 1, 16 * h, 16 * h + 16), None, T.mt[m:m + 16, :])
+    dma("y", "v", R("vt", 0, 512), None, T.v[:, :])
+
+    select(R("c0", 0, 512), R("ones", 0, 512), [[0, 8], [-16, 16], [1000, 4]], 0, 1)
+    select(R("ce", 0, 512), R("c0", 0, 512), [[0, 4], [1, 2], [0, 64]], 0, 0)
+    select(R("cd", 0, 512), R("c0", 0, 512), [[0, 4], [1, 2], [0, 64]], -1, 0)
+    for b in range(4):
+        select(R("e%d" % b, 0, 512), R("ones", 0, 512), [[1, 512]], -b, -4)
+
+    copy("v", R("mt16", 0, 24), R("mti", 0, 24))
+    quant("fq", 0, ROW, "fl", 0)
+    copy("v", R("offa", 0, 24), R("offi", 0, 24))
+    copy("s", R("r0", 0, C), R("idf", 0, C), R("offa", 0, 24))
+    copy("s", R("r0c", 0, C), R("r0", 0, C))
+    tt(R("wf", 0, C), R("idf", 0, C), R("idc", 0, C), OP.is_gt, R("mt16", 0, 24))
+    copy("s", R("wsg", 0, C), R("wf", 0, C), scale=2.0, bias=-1.0)
+    tt(R("dl8", 0, C), R("r0", 0, C), R("r0c", 0, C), OP.subtract, R("mt16", 0, 24))
+    for h in range(8):
+        o = 16 * (1 - h % 2)
+        dma("s", "bs", R("base", o, o + C, 1, 16 * h, 16 * h + 8), R("r0", 0, C, 1, 0, 128, 16))
+    for h in range(8):
+        o = 16 * (1 - h % 2)
+        dma("y", "dl", R("delta", o, o + C, 1, 16 * h, 16 * h + 8), R("dl8", 0, C, 1, 0, 128, 16))
+    quant("uq", 0, 128, "ut", 0)
+
+    def scores(k):
+        a, b = chunks[k]
+        mm(k, HALF, "uq", 0, "xq", a)
+
+    for k, (a, b) in enumerate(chunks):
+        quant("xq", a, b, "xt", 4 * a)
+        scores(k)
+
+    def gather(out, win, off, who="vs"):
+        if "v" in who:
+            copy("v", R(out, 16, 16 + 16 * NV), R(win, 16, ROW), R(off, 0, NV))
+        if "s" in who:
+            copy("s", R(out, 16 + 16 * NV, ROW), R(win, 16, ROW), R(off, NV, 25))
+
+    def place(off, k, slot):
+        ts(R(off, 0, 25), R("tr", ROW * k + 16 + slot, ROW * (k + 1), 16), P("cb"), None, OP.add)
+
+    for rnd, step in enumerate(STEP):
+        mate = T.cores[rank ^ step]
+        last = rnd == len(STEP) - 1
+        for k, (a, b) in enumerate(chunks):
+            tt(R("sw", a, b), R("ps%d" % k, 0, HALF), R("wsg", a, b), OP.mult)
+            copy("s", R("ns", a, b), R("sw", a, b), scale=-1.0)
+        if rnd == 0:
+            quant("ceq", 0, 128, "ce", 0)
+            quant("cdq", 0, 128, "cd", 0)
+        for k, (a, b) in enumerate(chunks):
+            tt(R("fl", 4 * (a + 16), 4 * (b + 16), 4), R("sw", 0, C), R("ns", a, b), OP.is_lt, R("mt16", a // 16, b // 16))
+            quant("fq", a + 16, b + 16, "fl", 4 * (a + 16))
+            n = HALF + 16 * k
+            mm(2 + k, n, "ceq", 0, "fq", a, True, False)
+            mm(2 + k, n, "cdq", 0, "fq", a + 16, False, True)
+        for t in range(4):
+            copy("s", R("xp%d" % t, 0, C), R("xt", t, 4 * C, 4))
+        for k in range(2):
+            a, b = (0, HALF) if k == 0 else (HALF, 400)
+            tt(R("tm", a, b), R("ps%d" % (2 + k), 0, b - a), R("delta", a, b), OP.mult)
+            tt(R("new", 16 + a, 16 + b), R("tm", a, b), R("base", a, b), OP.add)
+            if k == 0:
+                turn(R("tr", 0, HALF), R("new", 0, HALF))
+            else:
+                turn(R("tr", HALF, ROW), R("new", HALF, ROW))
+        place("ob", 0, 7)
+        gather("f1", "new", "ob")
+        place("oa", 0, 0)
+        turn(R("tr", ROW, ROW + HALF), R("f1", 0, HALF))
+        gather("f0", "new", "oa")
+        turn(R("tr", ROW + HALF, 2 * ROW), R("f1", HALF, ROW))
+        place("ok1", 1, 1)
+        for k in range(1, 7):
+            gather("pa", "f%d" % (k - 1), "ok%d" % k)
+            gather("f%d" % (k + 1), "pa", "ok%d" % k)
+            o = ROW * (k + 1)
+            turn(R("tr", o, o + HALF), R("f%d" % (k + 1), 0, HALF))
+            turn(R("tr", o + HALF, o + ROW), R("f%d" % (k + 1), HALF, ROW))
+            if k < 6:
+                place("ok%d" % (k + 1), k + 1, k + 1)
+        if last:
+            dma("y", "st", R("lb16", 0, C, 1, 0, 1), R("new", 32, ROW, 1, 0, 1))
+            for k in range(1, 8):
+                dma("y", "st", R("lb16", 0, C, 1, k, k + 1), R("f%d" % k, 32, ROW, 1, 8, 9))
+        else:
+            for s in (0, 7):
+                dma("y", "nb%d" % rnd, R("base", 0, 400, 1, s, 128, 16), R("new", 16, ROW, 1, s, 128, 16))
+        ts(R("lf", 0, 64), full, float(HALF), None, OP.add, None, R("sel", 0, 4))
+        remote(R("lr%d" % rnd, 0, 24), R("lf", 32, 56), mate, "ar%dl" % rnd, "lo%dl" % rnd, topo, core)
+        n = len(topo.engines(mate, core))
+        arrives(R("lr%d" % rnd, 0, 24), "ar%dl" % rnd, n)
+        for k, (a, b) in enumerate(chunks):
+            for t in range(4):
+                copy("vvss"[t], R("zt", 4 * a + t, 4 * b, 4), R("xp%d" % t, 0, C), R("lf", a // 16, b // 16))
+            quant("zq", a, b, "zt", 4 * a)
+            for i in (0, 2, 1, 3):
+                mm((4, 0)[k] + i, HALF, "wq", 128 * i, "zq", a)
+        for k, (a, b) in enumerate(chunks):
+            for i in (0, 2, 1, 3):
+                src, dst = R("ps%d" % ((4, 0)[k] + i), 0, HALF), R("hp%d" % i, a, b)
+                if i < 2:
+                    ts(dst, src, 0.03125, None, OP.mult)
+                else:
+                    copy("s", dst, src, scale=0.03125)
+        for k, (a, b) in enumerate(chunks):
+            for t in range(4):
+                copy("vvss"[t], R("hg", 4 * a + t, 4 * b, 4), R("hp%d" % t, 0, C), R("lr%d" % rnd, a // 16, b // 16))
+            quant("hq", a, b, "hg", 4 * a)
+            remote(B("hr%d" % rnd, a, b), B("hq", a, b), mate, "ar%dc%d" % (rnd, k), "lo%dc%d" % (rnd, k), topo, core)
+            remote(R("hr%ds" % rnd, a, b), R("hqs", a, b), mate, "ar%ds%d" % (rnd, k), "lo%ds%d" % (rnd, k), topo, core)
+        for k, (a, b) in enumerate(chunks):
+            arrives(R("hr%d" % rnd, a, b), "ar%dc%d" % (rnd, k), n)
+            arrives(R("hr%ds" % rnd, a, b), "ar%ds%d" % (rnd, k), n)
+        if rnd == 0:
+            for b in range(4):
+                quant("e%dq" % b, 0, 128, "e%d" % b, 0)
+            ts(R("ml", 0, 25), R("mi", 0, 25), P("cn"), None, OP.add)
+        if rnd == 1:
+            quant("vq", 0, 128, "vt", 0)
+        if not last:
+            copy("s", R("newc", 0, 400), R("new", 16, ROW))
+            tt(R("dab", 0, 400), R("new", 16, ROW), R("newc", 0, 400), OP.subtract, R("ml", 0, 25))
+            for s, p in ((0, 0), (7, 64)):
+                for h in (0, 64):
+                    dma("y", "nd%d" % rnd, R("delta", 0, 400, 1, h + s, h + 64, 16), R("dab", 0, 400, 1, p + s, p + 64, 16))
+        else:
+            copy("s", R("l32", 0, C, 1, 0, 8), R("lb16", 0, C, 1, 0, 8), bias=float(HALF))
+            dma("y", "out", None, R("l32", 0, C, 1, 0, 8), None, T.ll[:, :])
+        for k, (a, b) in enumerate(chunks):
+            for i in range(4):
+                mm((4, 0)[k] + i, HALF, "e%dq" % i, 0, "hr%d" % rnd, a)
+        for k, (a, b) in enumerate(chunks):
+            for i in range(4):
+                x = R("xt", 4 * a + i, 4 * b, 4)
+                tt(x, R("ps%d" % ((4, 0)[k] + i), 0, HALF), x, OP.add)
+            quant("xq", a, b, "xt", 4 * a)
+            if not last:
+                continue
+            dma("y", "out", None, B("xq", a, b), None, T.oc[:, 4 * a:4 * b])
+            for i in range(4):
+                dma("y", "out", None, R("xqs", a, b, 1, 32 * i, 32 * i + 4), None, T.osc[4 * i:4 * i + 4, a:b])
+            mm(4 + k, HALF, "vq", 0, "xq", a)
+            copy("s", R("ysb", a, b), R("ps%d" % (4 + k), 0, HALF))
+            dma("s", "out", None, R("ysb", a, b), None, T.y[:, a:b])
+        if not last:
+            for k in range(2):
+                scores(k)
+    finish()

@@ -2,19 +2,22 @@ from concourse.mybir import dt, AluOpType as OP, ActivationFunctionType as AF
 
 C = 384
 HALF = C // 2
+SCH = [(0, HALF), (HALF, C)]
+ZCH = [(0, 128), (128, 256), (256, 384)]
+NCH = [(0, 128), (128, 256), (256, 400)]
 STEP = [1, 2, 4]
 ROW = 416
 NV = 12
 
 SCRATCH = {}
-SEMAPHORES = ["cv", "cs", "ct", "cg"]
+SEMAPHORES = ["cv", "cs", "ct", "cg", "are", "loe"]
 
 
 def _declare():
     def sb(name, cols, dtype):
         SCRATCH[name] = ("sbuf", [128, cols], dtype)
     bf, f32, i32, u16, co, u8 = "bfloat16", "float32", "int32", "uint16", "float8_e4m3fn_x4", "uint8"
-    for n, c in (("xt", 4 * C), ("ut", 512), ("vt", 512), ("zt", 4 * C), ("hg", 4 * C), ("fl", 4 * ROW), ("ones", 512), ("c0", 512),
+    for n, c in (("xt", 4 * C), ("ut", 512), ("vt", 512), ("zt", 4 * C), ("hg", 4 * C), ("fl", 4 * ROW), ("ones", 512), ("onem", 512), ("c0", 512),
                  ("ce", 512), ("cd", 512), ("e0", 512), ("e1", 512), ("e2", 512), ("e3", 512), ("r0", C), ("r0c", C), ("newc", 400), ("idc", C), ("base", 400),
                  ("new", ROW), ("pa", ROW), ("tr", 8 * ROW), ("lb16", C)):
         sb(n, c, bf)
@@ -24,11 +27,11 @@ def _declare():
     for k in range(8):
         sb("f%d" % k, ROW, bf)
     for n, c in (("idf", 400), ("wsg", C), ("wf", C), ("dl8", C), ("delta", 400), ("tm", 400), ("dab", 400), ("sw", C), ("ns", C), ("ysb", C), ("l32", C),
-                 ("cb", 1), ("cn", 1), ("cm", 1), ("p15", 1), ("c32", 1), ("bs1", 1), ("t1", 1), ("t2", 1), ("bs2", 1), ("k2", 2)):
+                 ("cb", 1), ("cn", 1), ("cm", 1), ("p15", 1), ("c32", 1), ("bs1", 1), ("t1", 1), ("t2", 1), ("t3", 1), ("bs2", 1), ("k2", 2)):
         sb(n, c, f32)
-    for n, c in (("mti", 24), ("offi", 24), ("ip", 1), ("b16", 1), ("i15", 1), ("ph", 1), ("ik", 24), ("mi", 26)):
+    for n, c in (("mti", 24), ("offi", 24), ("ip", 1), ("b16", 1), ("i15", 1), ("ph", 1), ("ik", 2), ("mi", 26)):
         sb(n, c, i32)
-    for n, c in (("mt16", 24), ("offa", 24), ("sel", 4), ("ml", 26), ("oa", 26), ("ob", 26), ("lf", 64)):
+    for n, c in (("mt16", 24), ("offa", 24), ("sel", 6), ("ml", 26), ("oa", 26), ("ob", 26), ("lf", 96), ("le", 24), ("lm", 24)):
         sb(n, c, u16)
     for k in range(1, 7):
         sb("ok%d" % k, 26, u16)
@@ -46,7 +49,7 @@ def _declare():
         for n in ("l", "c0", "s0", "c1", "s1"):
             SEMAPHORES.append("ar%d%s" % (r, n))
             SEMAPHORES.append("lo%d%s" % (r, n))
-    for n in ("x0", "x1", "mt", "u", "v", "la", "wc", "ws", "mi", "bs", "dl", "st", "out"):
+    for n in ("x0", "x1", "mt", "u", "v", "la", "wc", "ws", "mi", "fl", "bs", "dl", "st", "out"):
         SEMAPHORES.append("d_" + n)
     for r in range(2):
         SEMAPHORES.append("d_nb%d" % r)
@@ -227,41 +230,70 @@ def rank_program(g, core, T, topo):
     dma("y", "mt", R("mti", 0, 24), None, T.mt[:, :])
     for k, (a, b) in enumerate(chunks):
         dma("y", "x%d" % k, R("xt", 4 * a, 4 * b), None, T.x[:, 4 * a:4 * b])
+    dma("s", "la", R("offi", 0, 24, 1, 0, 16), None, T.la[:, :])
+    dma("s", "la", R("offi", 0, 24, 1, 112, 128), None, T.lb[:, :])
+    dma("s", "la", R("offi", 0, 24, 1, 16, 112), None, T.mt[16:112, :])
     dma("s", "u", R("ut", 0, 512), None, T.u[:, :])
 
     iota(R("ip", 0, 1), [[0, 1]], 0, 1)
-    iota(R("ik", 0, 24), [[16, 24]], 0, 0)
+    iota(R("ik", 0, 2), [[16, 2]], 0, 0)
     iota(R("idf", 0, 400), [[1, 400]], -HALF, 0, True)
-    memset(R("ones", 0, 512), 1.0)
+    memset(R("fl", 0, ROW), 0.0)
+    for k in range(1, 4):
+        dma("y", "fl", R("fl", ROW * k, ROW * (k + 1)), R("fl", 0, ROW))
+    memset(R("onem", 0, 512), -1.0)
+    memset(R("onem", 0, 512, 64), 1.0)
+    memset(R("onem", 28, 512, 64), 1.0)
     ts(P("i15"), P("ip"), 15, None, OP.bitwise_and)
     ts(P("b16"), P("ip"), 16, None, OP.bitwise_and)
     ts(P("ph"), P("ip"), 4, None, OP.logical_shift_right)
     copy("v", P("p15"), P("i15"))
-    ts(R("offi", 0, 24), R("ik", 0, 24), P("p15"), None, OP.add)
-    dma("s", "la", R("offi", 0, 24, 1, 0, 16), None, T.la[:, :])
-    dma("s", "la", R("offi", 0, 24, 1, 112, 128), None, T.lb[:, :])
     ts(P("cb"), P("b16"), -1.0, 208.0, OP.mult, OP.add)
     ts(P("cm"), P("b16"), -16.0, None, OP.add)
     ts(P("cn"), P("b16"), -1.0, 16.0, OP.mult, OP.add)
     ts(P("c32"), P("b16"), -1.0, 32.0, OP.mult, OP.add)
-    ts(P("bs1"), P("ph"), float(ROW), P("c32"), OP.mult, OP.add)
-    ts(P("bs2"), P("ph"), -float(ROW), P("c32"), OP.mult, OP.add)
-    ts(P("bs2"), P("bs2"), 7.0 * ROW, None, OP.add)
+    memset(R("delta", 0, 400), 0.0)
+    memset(R("ones", 0, 512), 1.0)
     ts(P("t1"), P("ph"), 0.0, 8.0, OP.is_gt, OP.mult)
     ts(P("t2"), P("ph"), 7.0, 8.0, OP.is_lt, OP.mult)
-    tt(P("bs1"), P("bs1"), P("t1"), OP.add)
-    tt(P("bs2"), P("bs2"), P("t2"), OP.add)
+    ts(P("t3"), P("ph"), 6.0, 7.0, OP.is_equal, OP.mult)
+    ts(P("bs1"), P("ph"), float(ROW), P("c32"), OP.mult, OP.add)
+    ts(P("bs2"), P("ph"), -float(ROW), 7.0 * ROW, OP.mult, OP.add)
     ts(R("k2", 0, 2), R("ik", 0, 2), P("p15"), 23.0, OP.add, OP.min)
-    ts(R("sel", 0, 2), R("k2", 0, 2), 16.0, P("bs1"), OP.mult, OP.add)
-    ts(R("sel", 2, 4), R("k2", 0, 2), 16.0, P("bs2"), OP.mult, OP.add)
     copy("s", R("idc", 0, C), R("idf", 0, C))
     copy("s", R("base", 0, 400), R("idf", 0, 400), bias=P("cm"))
-    memset(R("delta", 0, 400), 0.0)
     memset(R("mi", 0, 26), 0)
-    memset(R("fl", 0, 4 * ROW), 0.0)
     memset(R("new", 0, 16), 0.0)
-    for k in range(1, 8):
-        memset(R("f%d" % k, 0, 16), 0.0)
+    memset(R("f1", 0, 16), 0.0)
+    select(R("c0", 0, 512), R("onem", 0, 512), [[0, 8], [-16, 16], [1000, 4]], 0, 1)
+    select(R("ce", 0, 512), R("c0", 0, 512), [[0, 4], [1, 2], [0, 64]], 0, 0)
+    select(R("cd", 0, 512), R("c0", 0, 512), [[0, 4], [1, 2], [0, 64]], -1, 0)
+    for b in range(4):
+        select(R("e%d" % b, 0, 512), R("ones", 0, 512), [[1, 512]], -b, -4)
+
+    copy("v", R("mt16", 0, 24), R("mti", 0, 24))
+    copy("v", R("offa", 0, 24), R("offi", 0, 24))
+    copy("s", R("r0", 0, C), R("idf", 0, C), R("offa", 0, 24))
+    tt(R("wf", 0, C), R("idf", 0, C), R("idc", 0, C), OP.is_gt, R("mt16", 0, 24))
+    copy("s", R("wsg", 0, C), R("wf", 0, C), scale=2.0, bias=-1.0)
+    for s, p in ((0, 0), (7, 112)):
+        for h in (0, 16):
+            dma("y", "bs", R("base", 16 - h, 16 - h + C, 1, h + s, 128, 32), R("r0", 0, C, 1, p, p + 4))
+    quant("uq", 0, 128, "ut", 0)
+
+    def scores(k):
+        a, b = chunks[k]
+        mm(k, HALF, "uq", 0, "xq", a)
+
+    copy("v", R("r0c", 0, C), R("r0", 0, C))
+    for k, (a, b) in enumerate(chunks):
+        quant("xq", a, b, "xt", 4 * a)
+        scores(k)
+        if k == 0:
+            tt(R("dl8", 0, C), R("r0", 0, C), R("r0c", 0, C), OP.subtract, R("mt16", 0, 24))
+    for h in range(8):
+        o = 16 * (1 - h % 2)
+        dma("ys"[h % 2], "dl", R("delta", o, o + C, 1, 16 * h, 16 * h + 8), R("dl8", 0, C, 1, 0, 128, 16))
     dma("y", "wc", ("wq", (0, 512, 1), (0, 128, 1), True), None, T.wc[:, :])
     dma("y", "ws", R("wqs", 0, 512), None, T.ws[:, :])
     for h in range(8):
@@ -270,41 +302,9 @@ def rank_program(g, core, T, topo):
         dma("y", "mi", R("mi", o, o + 24, 1, 16 * h, 16 * h + 16), None, T.mt[m:m + 16, :])
     dma("y", "v", R("vt", 0, 512), None, T.v[:, :])
 
-    select(R("c0", 0, 512), R("ones", 0, 512), [[0, 8], [-16, 16], [1000, 4]], 0, 1)
-    select(R("ce", 0, 512), R("c0", 0, 512), [[0, 4], [1, 2], [0, 64]], 0, 0)
-    select(R("cd", 0, 512), R("c0", 0, 512), [[0, 4], [1, 2], [0, 64]], -1, 0)
-    for b in range(4):
-        select(R("e%d" % b, 0, 512), R("ones", 0, 512), [[1, 512]], -b, -4)
-
-    copy("v", R("mt16", 0, 24), R("mti", 0, 24))
-    quant("fq", 0, ROW, "fl", 0)
-    copy("v", R("offa", 0, 24), R("offi", 0, 24))
-    copy("s", R("r0", 0, C), R("idf", 0, C), R("offa", 0, 24))
-    copy("s", R("r0c", 0, C), R("r0", 0, C))
-    tt(R("wf", 0, C), R("idf", 0, C), R("idc", 0, C), OP.is_gt, R("mt16", 0, 24))
-    copy("s", R("wsg", 0, C), R("wf", 0, C), scale=2.0, bias=-1.0)
-    tt(R("dl8", 0, C), R("r0", 0, C), R("r0c", 0, C), OP.subtract, R("mt16", 0, 24))
-    for h in range(8):
-        o = 16 * (1 - h % 2)
-        dma("s", "bs", R("base", o, o + C, 1, 16 * h, 16 * h + 8), R("r0", 0, C, 1, 0, 128, 16))
-    for h in range(8):
-        o = 16 * (1 - h % 2)
-        dma("y", "dl", R("delta", o, o + C, 1, 16 * h, 16 * h + 8), R("dl8", 0, C, 1, 0, 128, 16))
-    quant("uq", 0, 128, "ut", 0)
-
-    def scores(k):
-        a, b = chunks[k]
-        mm(k, HALF, "uq", 0, "xq", a)
-
-    for k, (a, b) in enumerate(chunks):
-        quant("xq", a, b, "xt", 4 * a)
-        scores(k)
-
-    def gather(out, win, off, who="vs"):
-        if "v" in who:
-            copy("v", R(out, 16, 16 + 16 * NV), R(win, 16, ROW), R(off, 0, NV))
-        if "s" in who:
-            copy("s", R(out, 16 + 16 * NV, ROW), R(win, 16, ROW), R(off, NV, 25))
+    def gather(out, win, off, m=NV):
+        copy("v", R(out, 16, 16 + 16 * m), R(win, 16, ROW), R(off, 0, m))
+        copy("s", R(out, 16 + 16 * m, ROW), R(win, 16, ROW), R(off, m, 25))
 
     def place(off, k, slot):
         ts(R(off, 0, 25), R("tr", ROW * k + 16 + slot, ROW * (k + 1), 16), P("cb"), None, OP.add)
@@ -318,28 +318,62 @@ def rank_program(g, core, T, topo):
         if rnd == 0:
             quant("ceq", 0, 128, "ce", 0)
             quant("cdq", 0, 128, "cd", 0)
-        for k, (a, b) in enumerate(chunks):
+        def flags(k):
+            a, b = ZCH[k]
             tt(R("fl", 4 * (a + 16), 4 * (b + 16), 4), R("sw", 0, C), R("ns", a, b), OP.is_lt, R("mt16", a // 16, b // 16))
-            quant("fq", a + 16, b + 16, "fl", 4 * (a + 16))
-            n = HALF + 16 * k
-            mm(2 + k, n, "ceq", 0, "fq", a, True, False)
-            mm(2 + k, n, "cdq", 0, "fq", a + 16, False, True)
+
+        def spread(k):
+            a, b = ((0, 144), (144, 272), (272, ROW))[k]
+            quant("fq", a, b, "fl", 4 * a)
+            a, b = NCH[k]
+            mm(2 + k, b - a, "ceq", 0, "fq", a, True, False)
+            mm(2 + k, b - a, "cdq", 0, "fq", a + 16, False, True)
+
+        flags(0)
+        flags(1)
+        spread(0)
+        flags(2)
+        spread(1)
+        spread(2)
         for t in range(4):
             copy("s", R("xp%d" % t, 0, C), R("xt", t, 4 * C, 4))
-        for k in range(2):
-            a, b = (0, HALF) if k == 0 else (HALF, 400)
+        if rnd == 0:
+            tt(P("t3"), P("t3"), P("c32"), OP.add)
+            tt(P("t2"), P("t2"), P("c32"), OP.add)
+            tt(P("bs1"), P("bs1"), P("t1"), OP.add)
+            tt(P("bs2"), P("bs2"), P("t2"), OP.add)
+            ts(R("sel", 0, 2), R("k2", 0, 2), 16.0, P("bs1"), OP.mult, OP.add)
+            ts(R("sel", 2, 4), R("k2", 0, 2), 16.0, P("bs2"), OP.mult, OP.add)
+            ts(R("sel", 4, 6), R("k2", 0, 2), 16.0, P("t3"), OP.mult, OP.add)
+            for k in range(2, 8):
+                copy("s", R("f%d" % k, 0, 16), R("new", 0, 16))
+
+        def change(k):
+            a, b = NCH[k]
             tt(R("tm", a, b), R("ps%d" % (2 + k), 0, b - a), R("delta", a, b), OP.mult)
+
+        def renew(k):
+            a, b = NCH[k]
             tt(R("new", 16 + a, 16 + b), R("tm", a, b), R("base", a, b), OP.add)
-            if k == 0:
-                turn(R("tr", 0, HALF), R("new", 0, HALF))
-            else:
-                turn(R("tr", HALF, ROW), R("new", HALF, ROW))
+
+        change(0)
+        change(1)
+        renew(0)
+        change(2)
+        renew(1)
+        renew(2)
+        turn(R("tr", 0, 256), R("new", 0, 256))
+        turn(R("tr", 256, ROW), R("new", 256, ROW))
         place("ob", 0, 7)
         gather("f1", "new", "ob")
         place("oa", 0, 0)
         turn(R("tr", ROW, ROW + HALF), R("f1", 0, HALF))
-        gather("f0", "new", "oa")
         turn(R("tr", ROW + HALF, 2 * ROW), R("f1", HALF, ROW))
+        gather("f0", "new", "oa", 8)
+        if rnd == 0:
+            ts(R("lf", 64, 96), R("tr", 0, ROW), float(HALF), None, OP.add, None, R("sel", 4, 6))
+            remote(R("le", 0, 24), R("lf", 64, 88), mate, "are", "loe", topo, core)
+            arrives(R("le", 0, 24), "are", len(topo.engines(mate, core)))
         place("ok1", 1, 1)
         for k in range(1, 7):
             gather("pa", "f%d" % (k - 1), "ok%d" % k)
@@ -360,26 +394,60 @@ def rank_program(g, core, T, topo):
         remote(R("lr%d" % rnd, 0, 24), R("lf", 32, 56), mate, "ar%dl" % rnd, "lo%dl" % rnd, topo, core)
         n = len(topo.engines(mate, core))
         arrives(R("lr%d" % rnd, 0, 24), "ar%dl" % rnd, n)
-        for k, (a, b) in enumerate(chunks):
-            for t in range(4):
-                copy("vvss"[t], R("zt", 4 * a + t, 4 * b, 4), R("xp%d" % t, 0, C), R("lf", a // 16, b // 16))
+        def layer(k):
+            a, b = ZCH[k]
+            for i in (0, 2, 1, 3):
+                mm((4, 0)[k % 2] + i, b - a, "wq", 128 * i, "zq", a)
+
+        def result(k, i):
+            a, b = ZCH[k]
+            src, dst = R("ps%d" % ((4, 0)[k % 2] + i), 0, b - a), R("hp%d" % i, a, b)
+            if i < 2:
+                ts(dst, src, 0.03125, None, OP.mult)
+            else:
+                copy("s", dst, src, scale=0.03125)
+
+        def parts(k, t):
+            a, b = SCH[k]
+            copy("vvss"[t], R("hg", 4 * a + t, 4 * b, 4), R("hp%d" % t, 0, C), R("lm" if rnd == 0 else "lr%d" % rnd, a // 16, b // 16))
+
+        def zed(k, t):
+            a, b = ZCH[k]
+            copy("vvss"[t], R("zt", 4 * a + t, 4 * b, 4), R("xp%d" % t, 0, C), R("lf", a // 16, b // 16))
+
+        for t in range(4):
+            zed(0, t)
+        for k, (a, b) in enumerate(ZCH):
+            if k + 1 < len(ZCH):
+                zed(k + 1, 0)
+                zed(k + 1, 2)
+                zed(k + 1, 3)
             quant("zq", a, b, "zt", 4 * a)
+            if k + 1 < len(ZCH):
+                zed(k + 1, 1)
+            if k < 2:
+                layer(k)
+        for k in range(len(ZCH) - 1):
             for i in (0, 2, 1, 3):
-                mm((4, 0)[k] + i, HALF, "wq", 128 * i, "zq", a)
-        for k, (a, b) in enumerate(chunks):
-            for i in (0, 2, 1, 3):
-                src, dst = R("ps%d" % ((4, 0)[k] + i), 0, HALF), R("hp%d" % i, a, b)
-                if i < 2:
-                    ts(dst, src, 0.03125, None, OP.mult)
-                else:
-                    copy("s", dst, src, scale=0.03125)
-        for k, (a, b) in enumerate(chunks):
-            for t in range(4):
-                copy("vvss"[t], R("hg", 4 * a + t, 4 * b, 4), R("hp%d" % t, 0, C), R("lr%d" % rnd, a // 16, b // 16))
+                result(k, i)
+            if k == 0:
+                for j in range(2, len(ZCH)):
+                    layer(j)
+        if rnd == 0:
+            copy("v", R("lm", 0, 24, 1, 96, 128), R("le", 0, 24, 1, 96, 128))
+            copy("v", R("lm", 0, 24, 1, 0, 96), R("lr0", 0, 24, 1, 0, 96))
+        for i in (0, 2, 1, 3):
+            result(len(ZCH) - 1, i)
+        for i in (0, 2, 1, 3):
+            parts(0, i)
+        for k, (a, b) in enumerate(SCH):
+            if k:
+                for t in range(4):
+                    parts(k, t)
             quant("hq", a, b, "hg", 4 * a)
             remote(B("hr%d" % rnd, a, b), B("hq", a, b), mate, "ar%dc%d" % (rnd, k), "lo%dc%d" % (rnd, k), topo, core)
             remote(R("hr%ds" % rnd, a, b), R("hqs", a, b), mate, "ar%ds%d" % (rnd, k), "lo%ds%d" % (rnd, k), topo, core)
-        for k, (a, b) in enumerate(chunks):
+        for k, (a, b) in enumerate(SCH):
             arrives(R("hr%d" % rnd, a, b), "ar%dc%d" % (rnd, k), n)
             arrives(R("hr%ds" % rnd, a, b), "ar%ds%d" % (rnd, k), n)
         if rnd == 0:
@@ -400,10 +468,18 @@ def rank_program(g, core, T, topo):
         for k, (a, b) in enumerate(chunks):
             for i in range(4):
                 mm((4, 0)[k] + i, HALF, "e%dq" % i, 0, "hr%d" % rnd, a)
+        def grow(k, i):
+            a, b = chunks[k]
+            x = R("xt", 4 * a + i, 4 * b, 4)
+            tt(x, R("ps%d" % ((4, 0)[k] + i), 0, HALF), x, OP.add)
+
+        for i in range(4):
+            grow(0, i)
+        grow(1, 0)
         for k, (a, b) in enumerate(chunks):
-            for i in range(4):
-                x = R("xt", 4 * a + i, 4 * b, 4)
-                tt(x, R("ps%d" % ((4, 0)[k] + i), 0, HALF), x, OP.add)
+            if k:
+                for i in range(1, 4):
+                    grow(1, i)
             quant("xq", a, b, "xt", 4 * a)
             if not last:
                 continue

from concourse.mybir import dt, AluOpType as OP, ActivationFunctionType as AF

C = 384
HALF = C // 2
SCH = [(0, HALF), (HALF, C)]
ZCH = [(0, 128), (128, 256), (256, 384)]
NCH = [(0, 128), (128, 256), (256, 400)]
STEP = [1, 2, 4]
ROW = 416
NV = 12

SCRATCH = {}
SEMAPHORES = ["cv", "cs", "ct", "cg", "are", "loe"]


def _declare():
    def sb(name, cols, dtype):
        SCRATCH[name] = ("sbuf", [128, cols], dtype)
    bf, f32, i32, u16, co, u8 = "bfloat16", "float32", "int32", "uint16", "float8_e4m3fn_x4", "uint8"
    for n, c in (("xt", 4 * C), ("ut", 512), ("vt", 512), ("zt", 4 * C), ("hg", 4 * C), ("fl", 4 * ROW), ("ones", 512), ("onem", 512), ("c0", 512),
                 ("ce", 512), ("cd", 512), ("e0", 512), ("e1", 512), ("e2", 512), ("e3", 512), ("r0", C), ("r0c", C), ("newc", 400), ("idc", C), ("base", 400),
                 ("new", ROW), ("pa", ROW), ("tr", 8 * ROW), ("lb16", C)):
        sb(n, c, bf)
    for b in range(4):
        sb("xp%d" % b, C, bf)
        sb("hp%d" % b, C, bf)
    for k in range(8):
        sb("f%d" % k, ROW, bf)
    for n, c in (("idf", 400), ("wsg", C), ("wf", C), ("dl8", C), ("delta", 400), ("tm", 400), ("dab", 400), ("sw", C), ("ns", C), ("ysb", C), ("l32", C),
                 ("cb", 1), ("cn", 1), ("cm", 1), ("p15", 1), ("c32", 1), ("bs1", 1), ("t1", 1), ("t2", 1), ("t3", 1), ("bs2", 1), ("k2", 2)):
        sb(n, c, f32)
    for n, c in (("mti", 24), ("offi", 24), ("ip", 1), ("b16", 1), ("i15", 1), ("ph", 1), ("ik", 2), ("mi", 26)):
        sb(n, c, i32)
    for n, c in (("mt16", 24), ("offa", 24), ("sel", 6), ("ml", 26), ("oa", 26), ("ob", 26), ("lf", 96), ("le", 24), ("lm", 24)):
        sb(n, c, u16)
    for k in range(1, 7):
        sb("ok%d" % k, 26, u16)
    for n, c in (("xq", C), ("uq", 128), ("vq", 128), ("zq", C), ("hq", C), ("fq", ROW), ("wq", 512), ("ceq", 128), ("cdq", 128),
                 ("e0q", 128), ("e1q", 128), ("e2q", 128), ("e3q", 128)):
        sb(n, c, co)
        sb(n + "s", c, u8)
    for r in range(3):
        sb("lr%d" % r, 24, u16)
        sb("hr%d" % r, C, co)
        sb("hr%ds" % r, C, u8)
    for k in range(8):
        SCRATCH["ps%d" % k] = ("psum", [128, 512], f32)
    for r in range(3):
        for n in ("l", "c0", "s0", "c1", "s1"):
            SEMAPHORES.append("ar%d%s" % (r, n))
            SEMAPHORES.append("lo%d%s" % (r, n))
    for n in ("x0", "x1", "mt", "u", "v", "la", "wc", "ws", "mi", "fl", "bs", "dl", "st", "out"):
        SEMAPHORES.append("d_" + n)
    for r in range(2):
        SEMAPHORES.append("d_nb%d" % r)
        SEMAPHORES.append("d_nd%d" % r)


_declare()


def _span(a, b, s):
    return slice(a, b) if s == 1 else slice(a, b, s)


def _meet(a0, a1, s, b0, b1, t):
    if a0 >= b1 or b0 >= a1:
        return False
    return not (s == t and s > 1 and (a0 - b0) % s)


def _builder(g, T):
    eng = {"v": g.vector, "s": g.scalar, "t": g.tensor, "g": g, "y": g.sync}
    known = {q: {} for q in eng}
    hist, cnt, closed = {}, {}, set()
    serial = [0]

    def ap(r):
        name, c, p, bits = r
        p = slice(None) if p == (0, 128, 1) else _span(*p)
        a = T[name][p, _span(*c)]
        return a.bitcast(dt.uint8) if bits else a

    def deps(q, reads, writes, matmul=False):
        found = {}
        for refs, w in ((reads, False), (writes, True)):
            for name, c, p, bits in refs:
                psum = name[:2] == "ps"
                for (c2, p2, w2, tok, clk, q2, n) in hist.get(name, ()):
                    if psum:
                        if q2 == q and (q == "t" or not (w or w2)):
                            continue
                    else:
                        if not (w or w2):
                            continue
                        if not (_meet(*c, *c2) and _meet(*p, *p2)):
                            continue
                    found[n] = (tok, clk)
        return [found[n] for n in sorted(found, reverse=True)]

    def wait(q, toks):
        k = known[q]
        for (sem, val), clk in toks:
            if sem in closed or sem[:2] == "d_":
                val = cnt[sem]
                closed.add(sem)
            if k.get(sem, 0) >= val:
                continue
            eng[q].wait_ge(T.sem[sem], val)
            k[sem] = val
            for s2, v2 in clk.items():
                if k.get(s2, 0) < v2:
                    k[s2] = v2

    def note(q, reads, writes, tok):
        serial[0] += 1
        clk = dict(known[q])
        for refs, w in ((reads, False), (writes, True)):
            for name, c, p, bits in refs:
                h = hist.setdefault(name, [])
                if w and name[:2] != "ps":
                    h[:] = [e for e in h if not (c[0] <= e[0][0] and e[0][1] <= c[1] and c[2] == 1 and p == (0, 128, 1))]
                h.append((c, p, w, tok, clk, q, serial[0]))

    def issue(q, fn, reads, writes, sem=None, inc=1):
        wait(q, deps(q, reads, writes))
        sem = sem or "c" + q
        assert sem not in closed, sem
        cnt[sem] = cnt.get(sem, 0) + inc
        fn(eng[q]).then_inc(T.sem[sem], inc)
        note(q, reads, writes, (sem, cnt[sem]))

    def remote(out, src, dst, ars, los, topo, core):
        wait("g", deps("g", [src], []))
        rid, pid, _ = topo.addr(dst)
        n = len(topo.engines(core, dst))
        g.remote_dma(ap(out), ap(src), T.sem[ars], T.sem[los], pid, rid, topo.mask(core, dst))
        cnt[los] = n
        note("g", [src], [], (los, n))

    def arrives(out, sem, n):
        serial[0] += 1
        cnt[sem] = n
        hist.setdefault(out[0], []).append((out[1], out[2], True, (sem, n), {}, "remote", serial[0]))

    def finish():
        for sem in sorted(cnt):
            if known["g"].get(sem, 0) < cnt[sem]:
                g.wait_ge(T.sem[sem], cnt[sem])
                known["g"][sem] = cnt[sem]

    return ap, issue, remote, arrives, finish


def rank_program(g, core, T, topo):
    rank = T.rank_of(core)
    if rank is None:
        return
    ap, issue, remote, arrives, finish = _builder(g, T)

    def R(name, c0, c1, cs=1, p0=0, p1=128, ps=1):
        return (name, (c0, c1, cs), (p0, p1, ps), False)

    def B(name, c0, c1):
        return (name, (c0, c1, 1), (0, 128, 1), True)

    def P(name, p0=0, p1=128):
        return R(name, 0, 1, 1, p0, p1)

    def dma(q, sem, out, in_, ext_in=None, ext_out=None):
        issue(q, lambda e: e.dma_start(ext_out if ext_out is not None else ap(out), ext_in if ext_in is not None else ap(in_)),
              [in_] if in_ else [], [out] if out else [], "d_" + sem, 16)

    def val(s):
        return ap(s) if isinstance(s, tuple) else s

    def memset(r, c):
        issue("v", lambda e: e.memset(ap(r), c), [], [r])

    def tt(out, a, b, op, off=None):
        def fn(e):
            x = ap(a)
            return e.tensor_tensor(ap(out), x.indirect(ap(off)) if off else x, ap(b), op)
        issue("v", fn, [a, b] + ([off] if off else []), [out])

    def ts(out, a, s1, s2, op0, op1=None, off=None):
        def fn(e):
            x = ap(a)
            x = x.indirect(ap(off)) if off else x
            if op1 is None:
                return e.tensor_scalar(ap(out), x, val(s1), None, op0)
            return e.tensor_scalar(ap(out), x, val(s1), val(s2), op0, op1)
        issue("v", fn, [a] + [s for s in (s1, s2, off) if isinstance(s, tuple)], [out])

    def copy(q, out, a, off=None, scale=None, bias=None):
        def fn(e):
            x = ap(a)
            x = x.indirect(ap(off)) if off else x
            if q == "v":
                return e.tensor_copy(ap(out), x)
            if bias is not None:
                return e.activation(ap(out), x, AF.Identity, bias=val(bias), scale=1.0 if scale is None else scale)
            return e.activation(ap(out), x, AF.Copy) if scale is None else e.activation(ap(out), x, AF.Copy, scale=scale)
        issue(q, fn, [a] + [r for r in (off, bias) if isinstance(r, tuple)], [out])

    def turn(out, a):
        issue("v", lambda e: e.transpose(ap(out), ap(a)), [a], [out])

    def quant(name, c0, c1, tile, t0):
        q, s, t = R(name, c0, c1), R(name + "s", c0, c1), R(tile, t0, t0 + 4 * (c1 - c0))
        issue("v", lambda e: e.quantize_mx(ap(q), ap(s), ap(t)), [t], [q, s])

    def mm(bank, n, lhs, l0, rhs, c0, start=True, stop=True):
        out = R("ps%d" % bank, 0, n)
        a, sa, b, sb = R(lhs, l0, l0 + 128), R(lhs + "s", l0, l0 + 128), R(rhs, c0, c0 + n), R(rhs + "s", c0, c0 + n)
        issue("t", lambda e: e.matmul_mx(ap(out), ap(a), ap(sa), ap(b), ap(sb), start, stop), [a, sa, b, sb], [out])

    def iota(r, pattern, base, mult, flag=False):
        if flag:
            issue("g", lambda e: e.iota(ap(r), pattern, base, mult, allow_small_or_imprecise_dtypes=True), [], [r])
        else:
            issue("g", lambda e: e.iota(ap(r), pattern, base, mult), [], [r])

    def select(out, in_, pattern, base, mult):
        issue("g", lambda e: e.affine_select(ap(out), ap(in_), pattern, OP.is_equal, 0.0, base, mult), [in_], [out])

    full = R("tr", 0, 8 * ROW)
    chunks = [(0, HALF), (HALF, C)]

    dma("y", "mt", R("mti", 0, 24), None, T.mt[:, :])
    for k, (a, b) in enumerate(chunks):
        dma("y", "x%d" % k, R("xt", 4 * a, 4 * b), None, T.x[:, 4 * a:4 * b])
    dma("s", "la", R("offi", 0, 24, 1, 0, 16), None, T.la[:, :])
    dma("s", "la", R("offi", 0, 24, 1, 112, 128), None, T.lb[:, :])
    dma("s", "la", R("offi", 0, 24, 1, 16, 112), None, T.mt[16:112, :])
    dma("s", "u", R("ut", 0, 512), None, T.u[:, :])

    iota(R("ip", 0, 1), [[0, 1]], 0, 1)
    iota(R("ik", 0, 2), [[16, 2]], 0, 0)
    iota(R("idf", 0, 400), [[1, 400]], -HALF, 0, True)
    memset(R("fl", 0, ROW), 0.0)
    for k in range(1, 4):
        dma("y", "fl", R("fl", ROW * k, ROW * (k + 1)), R("fl", 0, ROW))
    memset(R("onem", 0, 512), -1.0)
    memset(R("onem", 0, 512, 64), 1.0)
    memset(R("onem", 28, 512, 64), 1.0)
    ts(P("i15"), P("ip"), 15, None, OP.bitwise_and)
    ts(P("b16"), P("ip"), 16, None, OP.bitwise_and)
    ts(P("ph"), P("ip"), 4, None, OP.logical_shift_right)
    copy("v", P("p15"), P("i15"))
    ts(P("cb"), P("b16"), -1.0, 208.0, OP.mult, OP.add)
    ts(P("cm"), P("b16"), -16.0, None, OP.add)
    ts(P("cn"), P("b16"), -1.0, 16.0, OP.mult, OP.add)
    ts(P("c32"), P("b16"), -1.0, 32.0, OP.mult, OP.add)
    memset(R("delta", 0, 400), 0.0)
    memset(R("ones", 0, 512), 1.0)
    ts(P("t1"), P("ph"), 0.0, 8.0, OP.is_gt, OP.mult)
    ts(P("t2"), P("ph"), 7.0, 8.0, OP.is_lt, OP.mult)
    ts(P("t3"), P("ph"), 6.0, 7.0, OP.is_equal, OP.mult)
    ts(P("bs1"), P("ph"), float(ROW), P("c32"), OP.mult, OP.add)
    ts(P("bs2"), P("ph"), -float(ROW), 7.0 * ROW, OP.mult, OP.add)
    ts(R("k2", 0, 2), R("ik", 0, 2), P("p15"), 23.0, OP.add, OP.min)
    copy("s", R("idc", 0, C), R("idf", 0, C))
    copy("s", R("base", 0, 400), R("idf", 0, 400), bias=P("cm"))
    memset(R("mi", 0, 26), 0)
    memset(R("new", 0, 16), 0.0)
    memset(R("f1", 0, 16), 0.0)
    select(R("c0", 0, 512), R("onem", 0, 512), [[0, 8], [-16, 16], [1000, 4]], 0, 1)
    select(R("ce", 0, 512), R("c0", 0, 512), [[0, 4], [1, 2], [0, 64]], 0, 0)
    select(R("cd", 0, 512), R("c0", 0, 512), [[0, 4], [1, 2], [0, 64]], -1, 0)
    for b in range(4):
        select(R("e%d" % b, 0, 512), R("ones", 0, 512), [[1, 512]], -b, -4)

    copy("v", R("mt16", 0, 24), R("mti", 0, 24))
    copy("v", R("offa", 0, 24), R("offi", 0, 24))
    copy("s", R("r0", 0, C), R("idf", 0, C), R("offa", 0, 24))
    tt(R("wf", 0, C), R("idf", 0, C), R("idc", 0, C), OP.is_gt, R("mt16", 0, 24))
    copy("s", R("wsg", 0, C), R("wf", 0, C), scale=2.0, bias=-1.0)
    for s, p in ((0, 0), (7, 112)):
        for h in (0, 16):
            dma("y", "bs", R("base", 16 - h, 16 - h + C, 1, h + s, 128, 32), R("r0", 0, C, 1, p, p + 4))
    quant("uq", 0, 128, "ut", 0)

    def scores(k):
        a, b = chunks[k]
        mm(k, HALF, "uq", 0, "xq", a)

    copy("v", R("r0c", 0, C), R("r0", 0, C))
    for k, (a, b) in enumerate(chunks):
        quant("xq", a, b, "xt", 4 * a)
        scores(k)
        if k == 0:
            tt(R("dl8", 0, C), R("r0", 0, C), R("r0c", 0, C), OP.subtract, R("mt16", 0, 24))
    for h in range(8):
        o = 16 * (1 - h % 2)
        dma("ys"[h % 2], "dl", R("delta", o, o + C, 1, 16 * h, 16 * h + 8), R("dl8", 0, C, 1, 0, 128, 16))
    dma("y", "wc", ("wq", (0, 512, 1), (0, 128, 1), True), None, T.wc[:, :])
    dma("y", "ws", R("wqs", 0, 512), None, T.ws[:, :])
    for h in range(8):
        o = 1 - h % 2
        m = 0 if h < 4 else 112
        dma("y", "mi", R("mi", o, o + 24, 1, 16 * h, 16 * h + 16), None, T.mt[m:m + 16, :])
    dma("y", "v", R("vt", 0, 512), None, T.v[:, :])

    def gather(out, win, off, m=NV):
        copy("v", R(out, 16, 16 + 16 * m), R(win, 16, ROW), R(off, 0, m))
        copy("s", R(out, 16 + 16 * m, ROW), R(win, 16, ROW), R(off, m, 25))

    def place(off, k, slot):
        ts(R(off, 0, 25), R("tr", ROW * k + 16 + slot, ROW * (k + 1), 16), P("cb"), None, OP.add)

    for rnd, step in enumerate(STEP):
        mate = T.cores[rank ^ step]
        last = rnd == len(STEP) - 1
        for k, (a, b) in enumerate(chunks):
            tt(R("sw", a, b), R("ps%d" % k, 0, HALF), R("wsg", a, b), OP.mult)
            copy("s", R("ns", a, b), R("sw", a, b), scale=-1.0)
        if rnd == 0:
            quant("ceq", 0, 128, "ce", 0)
            quant("cdq", 0, 128, "cd", 0)
        def flags(k):
            a, b = ZCH[k]
            tt(R("fl", 4 * (a + 16), 4 * (b + 16), 4), R("sw", 0, C), R("ns", a, b), OP.is_lt, R("mt16", a // 16, b // 16))

        def spread(k):
            a, b = ((0, 144), (144, 272), (272, ROW))[k]
            quant("fq", a, b, "fl", 4 * a)
            a, b = NCH[k]
            mm(2 + k, b - a, "ceq", 0, "fq", a, True, False)
            mm(2 + k, b - a, "cdq", 0, "fq", a + 16, False, True)

        flags(0)
        flags(1)
        spread(0)
        flags(2)
        spread(1)
        spread(2)
        for t in range(4):
            copy("s", R("xp%d" % t, 0, C), R("xt", t, 4 * C, 4))
        if rnd == 0:
            tt(P("t3"), P("t3"), P("c32"), OP.add)
            tt(P("t2"), P("t2"), P("c32"), OP.add)
            tt(P("bs1"), P("bs1"), P("t1"), OP.add)
            tt(P("bs2"), P("bs2"), P("t2"), OP.add)
            ts(R("sel", 0, 2), R("k2", 0, 2), 16.0, P("bs1"), OP.mult, OP.add)
            ts(R("sel", 2, 4), R("k2", 0, 2), 16.0, P("bs2"), OP.mult, OP.add)
            ts(R("sel", 4, 6), R("k2", 0, 2), 16.0, P("t3"), OP.mult, OP.add)
            for k in range(2, 8):
                copy("s", R("f%d" % k, 0, 16), R("new", 0, 16))

        def change(k):
            a, b = NCH[k]
            tt(R("tm", a, b), R("ps%d" % (2 + k), 0, b - a), R("delta", a, b), OP.mult)

        def renew(k):
            a, b = NCH[k]
            tt(R("new", 16 + a, 16 + b), R("tm", a, b), R("base", a, b), OP.add)

        change(0)
        change(1)
        renew(0)
        change(2)
        renew(1)
        renew(2)
        turn(R("tr", 0, 256), R("new", 0, 256))
        turn(R("tr", 256, ROW), R("new", 256, ROW))
        place("ob", 0, 7)
        gather("f1", "new", "ob")
        place("oa", 0, 0)
        turn(R("tr", ROW, ROW + HALF), R("f1", 0, HALF))
        turn(R("tr", ROW + HALF, 2 * ROW), R("f1", HALF, ROW))
        gather("f0", "new", "oa", 8)
        if rnd == 0:
            ts(R("lf", 64, 96), R("tr", 0, ROW), float(HALF), None, OP.add, None, R("sel", 4, 6))
            remote(R("le", 0, 24), R("lf", 64, 88), mate, "are", "loe", topo, core)
            arrives(R("le", 0, 24), "are", len(topo.engines(mate, core)))
        place("ok1", 1, 1)
        for k in range(1, 7):
            gather("pa", "f%d" % (k - 1), "ok%d" % k)
            gather("f%d" % (k + 1), "pa", "ok%d" % k)
            o = ROW * (k + 1)
            turn(R("tr", o, o + HALF), R("f%d" % (k + 1), 0, HALF))
            turn(R("tr", o + HALF, o + ROW), R("f%d" % (k + 1), HALF, ROW))
            if k < 6:
                place("ok%d" % (k + 1), k + 1, k + 1)
        if last:
            dma("y", "st", R("lb16", 0, C, 1, 0, 1), R("new", 32, ROW, 1, 0, 1))
            for k in range(1, 8):
                dma("y", "st", R("lb16", 0, C, 1, k, k + 1), R("f%d" % k, 32, ROW, 1, 8, 9))
        else:
            for s in (0, 7):
                dma("y", "nb%d" % rnd, R("base", 0, 400, 1, s, 128, 16), R("new", 16, ROW, 1, s, 128, 16))
        ts(R("lf", 0, 64), full, float(HALF), None, OP.add, None, R("sel", 0, 4))
        remote(R("lr%d" % rnd, 0, 24), R("lf", 32, 56), mate, "ar%dl" % rnd, "lo%dl" % rnd, topo, core)
        n = len(topo.engines(mate, core))
        arrives(R("lr%d" % rnd, 0, 24), "ar%dl" % rnd, n)
        def layer(k):
            a, b = ZCH[k]
            for i in (0, 2, 1, 3):
                mm((4, 0)[k % 2] + i, b - a, "wq", 128 * i, "zq", a)

        def result(k, i):
            a, b = ZCH[k]
            src, dst = R("ps%d" % ((4, 0)[k % 2] + i), 0, b - a), R("hp%d" % i, a, b)
            if i < 2:
                ts(dst, src, 0.03125, None, OP.mult)
            else:
                copy("s", dst, src, scale=0.03125)

        def parts(k, t):
            a, b = SCH[k]
            copy("vvss"[t], R("hg", 4 * a + t, 4 * b, 4), R("hp%d" % t, 0, C), R("lm" if rnd == 0 else "lr%d" % rnd, a // 16, b // 16))

        def zed(k, t):
            a, b = ZCH[k]
            copy("vvss"[t], R("zt", 4 * a + t, 4 * b, 4), R("xp%d" % t, 0, C), R("lf", a // 16, b // 16))

        for t in range(4):
            zed(0, t)
        for k, (a, b) in enumerate(ZCH):
            if k + 1 < len(ZCH):
                zed(k + 1, 0)
                zed(k + 1, 2)
                zed(k + 1, 3)
            quant("zq", a, b, "zt", 4 * a)
            if k + 1 < len(ZCH):
                zed(k + 1, 1)
            if k < 2:
                layer(k)
        for k in range(len(ZCH) - 1):
            for i in (0, 2, 1, 3):
                result(k, i)
            if k == 0:
                for j in range(2, len(ZCH)):
                    layer(j)
        if rnd == 0:
            copy("v", R("lm", 0, 24, 1, 96, 128), R("le", 0, 24, 1, 96, 128))
            copy("v", R("lm", 0, 24, 1, 0, 96), R("lr0", 0, 24, 1, 0, 96))
        for i in (0, 2, 1, 3):
            result(len(ZCH) - 1, i)
        for i in (0, 2, 1, 3):
            parts(0, i)
        for k, (a, b) in enumerate(SCH):
            if k:
                for t in range(4):
                    parts(k, t)
            quant("hq", a, b, "hg", 4 * a)
            remote(B("hr%d" % rnd, a, b), B("hq", a, b), mate, "ar%dc%d" % (rnd, k), "lo%dc%d" % (rnd, k), topo, core)
            remote(R("hr%ds" % rnd, a, b), R("hqs", a, b), mate, "ar%ds%d" % (rnd, k), "lo%ds%d" % (rnd, k), topo, core)
        for k, (a, b) in enumerate(SCH):
            arrives(R("hr%d" % rnd, a, b), "ar%dc%d" % (rnd, k), n)
            arrives(R("hr%ds" % rnd, a, b), "ar%ds%d" % (rnd, k), n)
        if rnd == 0:
            for b in range(4):
                quant("e%dq" % b, 0, 128, "e%d" % b, 0)
            ts(R("ml", 0, 25), R("mi", 0, 25), P("cn"), None, OP.add)
        if rnd == 1:
            quant("vq", 0, 128, "vt", 0)
        if not last:
            copy("s", R("newc", 0, 400), R("new", 16, ROW))
            tt(R("dab", 0, 400), R("new", 16, ROW), R("newc", 0, 400), OP.subtract, R("ml", 0, 25))
            for s, p in ((0, 0), (7, 64)):
                for h in (0, 64):
                    dma("y", "nd%d" % rnd, R("delta", 0, 400, 1, h + s, h + 64, 16), R("dab", 0, 400, 1, p + s, p + 64, 16))
        else:
            copy("s", R("l32", 0, C, 1, 0, 8), R("lb16", 0, C, 1, 0, 8), bias=float(HALF))
            dma("y", "out", None, R("l32", 0, C, 1, 0, 8), None, T.ll[:, :])
        for k, (a, b) in enumerate(chunks):
            for i in range(4):
                mm((4, 0)[k] + i, HALF, "e%dq" % i, 0, "hr%d" % rnd, a)
        def grow(k, i):
            a, b = chunks[k]
            x = R("xt", 4 * a + i, 4 * b, 4)
            tt(x, R("ps%d" % ((4, 0)[k] + i), 0, HALF), x, OP.add)

        for i in range(4):
            grow(0, i)
        grow(1, 0)
        for k, (a, b) in enumerate(chunks):
            if k:
                for i in range(1, 4):
                    grow(1, i)
            quant("xq", a, b, "xt", 4 * a)
            if not last:
                continue
            dma("y", "out", None, B("xq", a, b), None, T.oc[:, 4 * a:4 * b])
            for i in range(4):
                dma("y", "out", None, R("xqs", a, b, 1, 32 * i, 32 * i + 4), None, T.osc[4 * i:4 * i + 4, a:b])
            mm(4 + k, HALF, "vq", 0, "xq", a)
            copy("s", R("ysb", a, b), R("ps%d" % (4 + k), 0, HALF))
            dma("s", "out", None, R("ysb", a, b), None, T.y[:, a:b])
        if not last:
            for k in range(2):
                scores(k)
    finish()
